import numpy as np
import ml_dtypes


def mxq(x, axis, fmt="e4m3"):
    dtype, down = {"e4m3": (ml_dtypes.float8_e4m3fn, 7), "e5m2": (ml_dtypes.float8_e5m2, 14)}[fmt]
    v = np.moveaxis(np.asarray(x, np.float32).astype(ml_dtypes.bfloat16).astype(np.float64), axis, -1)
    blocks = v.reshape(v.shape[:-1] + (-1, 32))
    amax = np.abs(blocks).max(-1, keepdims=True)
    byte = np.maximum(np.where(amax > 0, np.frexp(amax)[1] - 1 + 127, 0) - down, 1)
    scale = np.exp2(byte - 127.0)
    codes = (blocks / scale).astype(np.float32).astype(dtype).astype(np.float64)
    return np.moveaxis((codes * scale).reshape(v.shape), -1, axis)


WIDE = False


def mx_kscale(k):
    if not WIDE:
        return np.ones(k)
    levels = np.array([10, -10, 5, -5, 0])
    if k % 512:
        return np.exp2(np.random.permutation(np.resize(levels, k // 32))).repeat(32)
    a = np.empty((k // 512, 16))
    for p in range(k // 512):
        a[p, :8] = np.random.permutation(np.resize(levels, 8))
        for g in range(8):
            far = levels[np.abs(levels - a[p, g]) >= 10]
            a[p, g + 8] = far[np.random.randint(len(far))]
    return np.exp2(a.ravel()).repeat(32)


def f64(x):
    return np.asarray(x).astype(np.float64)


def striped(idx):
    return np.tile(idx.reshape(-1, 16).T, (8, 1)).astype(np.uint16)


def unstriped(offs):
    return offs[:16].T.reshape(-1).astype(np.int64)


E2M1 = np.array([0.0, 0.5, 1.0, 1.5, 2.0, 3.0, 4.0, 6.0, -0.0, -0.5, -1.0, -1.5, -2.0, -3.0, -4.0, -6.0])


def pack_weight(w, fmt):
    k, n = w.shape
    w = f64(np.asarray(w, np.float32).astype(ml_dtypes.bfloat16)).reshape(k // 32, 32, n)
    amax = np.abs(w).max(1)
    if fmt == "e4m3":
        byte = np.frexp(amax)[1] - 1 + 127 - 7
    else:
        mant, ex = np.frexp(amax / 6.0)
        byte = np.where(mant > 0.5, ex, ex - 1) + 127
    byte = np.clip(np.where(amax > 0, byte, 1), 1, 254)
    scaled = (w * np.exp2(127.0 - byte)[:, None, :]).reshape(k, n).astype(np.float32)
    by_word = np.ascontiguousarray(scaled.reshape(k // 512, 128, 4, n).transpose(0, 1, 3, 2))
    if fmt == "e4m3":
        words = by_word.astype(ml_dtypes.float8_e4m3fn).view(np.uint8)
    else:
        c = by_word.astype(ml_dtypes.float4_e2m1fn).view(np.uint8) & 0xF
        words = (c[..., 0::2] | (c[..., 1::2] << 4)).reshape(k // 512, 128, 2 * n)
    return np.ascontiguousarray(words), np.ascontiguousarray(byte.astype(np.uint8).reshape(k // 512, 16, n))


def unpack_weight(words, scales, fmt):
    g, _, n = scales.shape
    words = np.ascontiguousarray(words).reshape(g, 128, n, -1)
    if fmt == "e4m3":
        vals = words.view(ml_dtypes.float8_e4m3fn).astype(np.float64)
    else:
        nib = np.empty((g, 128, n, 4), np.uint8)
        nib[..., 0::2] = words & 0xF
        nib[..., 1::2] = words >> 4
        vals = E2M1[nib]
    vals = vals * np.repeat(np.exp2(scales.astype(np.float64) - 127.0), 8, axis=1)[..., None]
    return vals.transpose(0, 1, 3, 2).reshape(g * 512, n)


def gelu(v):
    return 0.5 * v * (1.0 + np.tanh(np.sqrt(2.0 / np.pi) * (v + 0.044715 * v**3)))


def twice(P):
    return np.random.permutation(np.repeat(np.arange(P), 2))


K, H, T, S, P = 1536, 1024, 2048, 1024, 512

def setup_inputs():
    n = np.random.standard_normal
    s = mx_kscale(K)[:, None]
    u = mx_kscale(H)[:, None]
    d = {}
    d["tab_words"], d["tab_scales"] = pack_weight(n((K, T)) * s, "e4m3")
    d["offs"] = striped(np.random.permutation(T)[:S])
    d["w1"] = (n((K, H)) / s * u.T / K ** 0.5).astype(np.float32)
    d["b1"] = (0.6 * n(H) * u[:, 0]).astype(np.float32)
    d["pos1"] = striped(np.random.permutation(S)[:P])
    d["pos2"] = striped(np.random.permutation(S)[:P])
    d["pos3"] = striped(twice(P))
    d["w4_words"], d["w4_scales"] = pack_weight(n((H, H)) / u / H ** 0.5, "e2m1")
    d["gain"] = (np.random.uniform(0.5, 1.5, H) / u[:, 0]).astype(np.float32)
    return d

def reference(tab_words, tab_scales, offs, w1, b1, pos1, pos2, pos3, w4_words, w4_scales, gain):
    v = unpack_weight(tab_words, tab_scales, "e4m3")[:, unstriped(offs)]
    w1q = mxq(f64(w1), 0, "e4m3")
    h = (w1q.T @ v) + f64(b1)[:, None]
    x = np.maximum(h[:, unstriped(pos1)], h[:, unstriped(pos2)])
    xq = mxq(x, 0, "e4m3")
    w4 = unpack_weight(w4_words, w4_scales, "e2m1")
    y = w4.T @ xq
    up = y[:, unstriped(pos3)]
    out = np.maximum(up, f64(gain)[:, None] * h)
    return out

@@ -1,0 +1,252 @@
+import itertools
+from contextlib import ExitStack
+
+import concourse.mybir as mybir
+
+K, H, T, S, V = 1536, 1024, 2048, 1024, 512
+FLOPS = 2 * K * H * S + 2 * H * H * V
+
+F32 = mybir.dt.float32
+BF16 = mybir.dt.bfloat16
+I32 = mybir.dt.int32
+U32 = mybir.dt.uint32
+U16 = mybir.dt.uint16
+U8 = mybir.dt.uint8
+FP8X4 = mybir.dt.float8_e4m3fn_x4
+FP4X4 = mybir.dt.float4_e2m1fn_x4
+ALU = mybir.AluOpType
+ACT = mybir.ActivationFunctionType
+
+P = 128
+PACK = 4
+KP = P * PACK
+BANK = 512
+Y_WINDOW = 1408
+Y_TILES = 3
+
+
+def tile_list_village_trap_peaks_kernel(
+    tc, tab_words, tab_scales, offs, w1, b1, pos1, pos2, pos3, w4_words, w4_scales, gain, out
+):
+    nc = tc.nc
+    k_passes = K // KP
+    r_passes = H // KP
+    halves = S // BANK
+
+    with ExitStack() as ctx:
+        keep = ctx.enter_context(tc.tile_pool(name="keep", bufs=1))
+        ring = ctx.enter_context(tc.tile_pool(name="ring", bufs=2))
+        psum = ctx.enter_context(tc.psum_pool(name="psum", bufs=8))
+
+        def load_list(src, name):
+            dst = keep.tile(list(src.shape), U16, name=name)
+            nc.sync.dma_start(dst[:], src)
+            return dst
+
+        tab_sc = keep.tile([P, T], U8, align_bytes=64)
+        nc.vector.memset(tab_sc[:].bitcast(I32), 0)
+        w4_sc = keep.tile([P, r_passes * H], U8, align_bytes=64)
+        nc.vector.memset(w4_sc[:].bitcast(I32), 0)
+        y_tiles = [keep.tile([P, Y_WINDOW], F32, name=f"y{i}") for i in range(Y_TILES)]
+        for y in y_tiles:
+            nc.vector.memset(y[:, V:], 0.0)
+
+        warm = keep.tile([P, 1], F32)
+        nc.scalar.activation(warm[:], y_tiles[0][:, V : V + 1], ACT.Identity)
+
+        offs_sb = load_list(offs, "offs_sb")
+        tab_w = [keep.tile([P, T], I32, name=f"tab_w{a}") for a in range(k_passes)]
+
+        def load_tab(a):
+            nc.sync.dma_start(tab_w[a][:], tab_words[a].rearrange("p n i -> p (n i)").bitcast(I32))
+
+        def load_w1(a, c0, width):
+            raw = ring.tile([P, PACK, width], F32, tag="raw", bufs=5, name="raw")
+            rows = w1[a * KP : (a + 1) * KP, c0 : c0 + width]
+            nc.sync.dma_start(raw[:], rows.rearrange("(p j) c -> p j c", j=PACK))
+            return raw
+
+        load_tab(0)
+        raw00 = load_w1(0, 0, KP)
+        sc_in = keep.tile([P, T // 4], I32)
+        for q in range(4):
+            live = slice(32 * q, 32 * q + 4 * k_passes)
+            nc.sync.dma_start(sc_in[live, :], tab_scales[:, 4 * q : 4 * q + 4, :].bitcast(I32))
+            nc.vector.tensor_copy(tab_sc[live, :].bitcast(I32), sc_in[live, :])
+        load_tab(1)
+        raw01 = load_w1(1, 0, KP)
+        load_tab(2)
+        b1_sb = [ring.tile([P, PACK], F32, tag=f"woven{1 - b}", bufs=1, align_bytes=64, name="b1_sb") for b in range(r_passes)]
+
+        def load_b1(b):
+            nc.sync.dma_start(b1_sb[b][:], b1[b * KP : (b + 1) * KP].rearrange("(p t) -> p t", t=PACK))
+
+        load_b1(0)
+        raw02 = [load_w1(2, i * 256, 256) for i in range(2)]
+        pos1_sb = load_list(pos1, "pos1_sb")
+        pos2_sb = load_list(pos2, "pos2_sb")
+
+        v_w = [keep.tile([P, S], U32, name=f"v_w{a}", align_bytes=64) for a in range(k_passes)]
+        v_sc = keep.tile([P, S], U8, align_bytes=64)
+        for a in range(k_passes):
+            nc.vector.tensor_copy(v_w[a][:], tab_w[a][:].bitcast(U32).indirect(offs_sb[:]))
+            if a == 0:
+                nc.vector.tensor_copy(v_sc[:], tab_sc[:].indirect(offs_sb[:]))
+
+        def weave_w1(copy, dealt, raw, m0):
+            width = raw.shape[2]
+            dst = dealt[:].rearrange("p (t m j) -> p m j t", t=PACK, j=PACK)
+            copy(dst[:, m0 : m0 + width // PACK], raw.rearrange("p j (m t) -> p m j t", t=PACK))
+
+        def new_dealt(b, a):
+            return ring.tile([P, PACK * KP], BF16, tag=f"dealt{a}", bufs=1, align_bytes=64, name="dealt")
+
+        def quantise(src, cols, name, cuts=None):
+            codes = keep.tile([P, cols], U32, name=name + "_c", align_bytes=64)
+            scales = keep.tile([P, cols], U8, name=name + "_s", align_bytes=64)
+            cuts = cuts or (0, cols)
+            for c0, c1 in zip(cuts, cuts[1:]):
+                nc.vector.quantize_mx(
+                    out=codes[:, c0:c1].bitcast(FP8X4), scales=scales[:, c0:c1], in_=src[:, PACK * c0 : PACK * c1]
+                )
+            return codes, scales
+
+        def first_stage(acc, wq):
+            for t in range(PACK):
+                for a, n in itertools.product(range(k_passes), range(halves)):
+                    codes, scales = wq[a]
+                    cols = slice(n * BANK, (n + 1) * BANK)
+                    nc.tensor.matmul_mx(
+                        out=acc[t][n][:],
+                        lhsT=codes[:, t * P : (t + 1) * P].bitcast(FP8X4),
+                        lhsT_scale=scales[:, t * P : (t + 1) * P],
+                        rhs=v_w[a][:, cols].bitcast(FP8X4),
+                        rhs_scale=v_sc[4 * a : P, cols],
+                        start=(a == 0),
+                        stop=(a == k_passes - 1),
+                    )
+
+        def new_acc():
+            return [[psum.tile([P, BANK], F32, tag="acc", name="acc") for n in range(halves)] for t in range(PACK)]
+
+        h_rows = [keep.tile([P, S], F32, name=f"h_rows{c}") for c in range(H // P)]
+
+        def leave_psum(acc, b, t):
+            h = ring.tile([P, S], F32, tag="h", bufs=6, name="h")
+            bias = b1_sb[b][:, t : t + 1]
+            for n in range(halves):
+                dst = h[:, n * BANK : (n + 1) * BANK]
+                if b == 0 and t == 0:
+                    nc.vector.tensor_scalar(dst, acc[t][n][:], bias, None, ALU.add)
+                else:
+                    nc.scalar.activation(dst, acc[t][n][:], ACT.Identity, bias=bias)
+            for u in range(PACK):
+                nc.sync.dma_start(h_rows[PACK * b + u][t:P:PACK, :], h[32 * u : 32 * (u + 1), :])
+            return h
+
+        def pick(h_pair, x_planes, t0, m0, m1, second_tag, first_tag=None):
+            width = m1 - m0
+            entries = slice(m0 // 16, m1 // 16)
+            if first_tag is None:
+                first = ring.tile([P, 2, width], F32, tag="first", name="first")
+            else:
+                first = ring.tile([P, 2, width], F32, tag=first_tag, bufs=1, align_bytes=64, name="first")
+            if second_tag is None:
+                second = ring.tile([P, 2, width], F32, tag="second", name="second")
+            else:
+                second = ring.tile([P, 2, width], F32, tag=second_tag, bufs=1, align_bytes=64, name="second")
+            for i in range(2):
+                nc.vector.tensor_copy(first[:, i, :], h_pair[i][:].indirect(pos1_sb[:, entries]))
+                nc.vector.tensor_copy(second[:, i, :], h_pair[i][:].indirect(pos2_sb[:, entries]))
+            nc.vector.tensor_tensor(x_planes[:, t0 : t0 + 2, m0:m1], first[:], second[:], ALU.max)
+
+        def weave_x(copy, woven, x_planes, m0, m1):
+            dst = woven[:, PACK * m0 : PACK * m1].rearrange("p (c i t) -> p c t i", i=4, t=PACK)
+            copy(dst, x_planes[:, :, m0:m1].rearrange("p t (c i) -> p c t i", i=4))
+
+        acc0 = new_acc()
+        dealt = new_dealt(0, 0)
+        weave_w1(nc.scalar.copy, dealt, raw00[:], 0)
+        wq0 = [quantise(dealt, KP, "w00")]
+        dealt = new_dealt(0, 1)
+        weave_w1(nc.scalar.copy, dealt, raw01[:], 0)
+        wq0.append(quantise(dealt, KP, "w01"))
+        dealt = new_dealt(0, 2)
+        weave_w1(nc.scalar.copy, dealt, raw02[0][:], 0)
+        weave_w1(nc.scalar.copy, dealt, raw02[1][:], 64)
+        wq0.append(quantise(dealt, KP, "w02", (0, 128, 256, 512)))
+        first_stage(acc0, wq0)
+
+        raw1 = [load_w1(a, KP, KP) for a in range(k_passes)]
+        w4_w = [keep.tile([P, 2 * H], U8, name=f"w4_w{a}", align_bytes=64) for a in range(r_passes)]
+        for a in range(r_passes):
+            nc.sync.dma_start(w4_w[a][:].bitcast(I32), w4_words[a].bitcast(I32))
+        for q in range(4):
+            nc.sync.dma_start(
+                w4_sc[32 * q : 32 * q + 4, :].bitcast(I32).rearrange("p (a n) -> p a n", a=r_passes),
+                w4_scales[:, 4 * q : 4 * q + 4, :].bitcast(I32).rearrange("a r n -> r a n"),
+            )
+        load_b1(1)
+        pos3_sb = load_list(pos3, "pos3_sb")
+        gain_sb = keep.tile([P, H // P], F32)
+        with nc.allow_non_contiguous_dma(reason="one gain value a partition and tile"):
+            nc.sync.dma_start(gain_sb[:], gain.rearrange("(c p) -> p c", p=P))
+
+        x_planes = [ring.tile([P, PACK, V], BF16, tag="x_planes", name="x_planes") for b in range(r_passes)]
+        h0 = [leave_psum(acc0, 0, t) for t in range(PACK)]
+        pick(h0[0:2], x_planes[0], 0, 0, V, None)
+        wq1 = []
+        for a in range(k_passes):
+            dealt = new_dealt(1, a)
+            weave_w1(nc.scalar.copy, dealt, raw1[a][:], 0)
+            wq1.append(quantise(dealt, KP, f"w1{a}"))
+        acc1 = new_acc()
+        first_stage(acc1, wq1)
+        pick(h0[2:4], x_planes[0], 2, 0, V, "dealt2", "dealt1")
+
+        h1 = [leave_psum(acc1, 1, t) for t in range(PACK)]
+        pick(h1[0:2], x_planes[1], 0, 0, V, None)
+        woven0 = ring.tile([P, PACK * V], BF16, tag="woven0", bufs=1, align_bytes=64)
+        weave_x(nc.scalar.copy, woven0, x_planes[0], 0, V)
+        xq = [quantise(woven0, V, "x0")]
+
+        woven1 = ring.tile([P, PACK * V], BF16, tag="woven1", bufs=1, align_bytes=64)
+        x1_c = keep.tile([P, V], U32, align_bytes=64)
+        x1_s = keep.tile([P, V], U8, align_bytes=64)
+        half = V // 2
+        for i, copy in enumerate((nc.scalar.copy, nc.vector.tensor_copy)):
+            m0, m1 = i * half, (i + 1) * half
+            pick(h1[2:4], x_planes[1], 2, m0, m1, "woven0" if i == 0 else None)
+            weave_x(copy, woven1, x_planes[1], m0, m1)
+            nc.vector.quantize_mx(
+                out=x1_c[:, m0:m1].bitcast(FP8X4), scales=x1_s[:, m0:m1], in_=woven1[:, PACK * m0 : PACK * m1]
+            )
+        xq.append((x1_c, x1_s))
+
+        acc2 = [psum.tile([P, BANK], F32, tag="acc", name="acc") for c in range(H // P)]
+        for a in range(r_passes):
+            codes, scales = xq[a]
+            for c in range(H // P):
+                nc.tensor.matmul_mx(
+                    out=acc2[c][:],
+                    lhsT=w4_w[a][:, 2 * P * c : 2 * P * (c + 1)].bitcast(FP4X4),
+                    lhsT_scale=w4_sc[:, a * H + c * P : a * H + (c + 1) * P],
+                    rhs=codes[:].bitcast(FP8X4),
+                    rhs_scale=scales[:],
+                    start=(a == 0),
+                    stop=(a == r_passes - 1),
+                )
+
+        for c in range(H // P):
+            y = y_tiles[c % Y_TILES]
+            nc.scalar.copy(y[:, :V], acc2[c][:])
+            pieces = 2 if c == H // P - 1 else 1
+            width = S // pieces
+            for i in range(pieces):
+                cols = slice(i * width, (i + 1) * width)
+                up = ring.tile([P, width], F32, tag="up", bufs=3, name="up")
+                nc.vector.tensor_copy(up[:], y[:].indirect(pos3_sb[:, i * width // 16 : (i + 1) * width // 16]))
+                nc.vector.scalar_tensor_tensor(
+                    up[:], h_rows[c][:, cols], gain_sb[:, c : c + 1], up[:], ALU.mult, ALU.max
+                )
+                nc.sync.dma_start(out[c * P : (c + 1) * P, cols], up[:])

@@ -21,8 +21,12 @@ P = 128
 PACK = 4
 KP = P * PACK
 BANK = 512
+PAIR = 2 * P
 Y_WINDOW = 1408
 Y_TILES = 3
+LATE = 128
+EARLY = V - LATE
+LAST_CUTS = (0, 512, 768, 1024)
 
 
 def tile_list_village_trap_peaks_kernel(
@@ -32,16 +36,20 @@ def tile_list_village_trap_peaks_kernel(
     k_passes = K // KP
     r_passes = H // KP
     halves = S // BANK
+    tiles = H // P
 
     with ExitStack() as ctx:
         keep = ctx.enter_context(tc.tile_pool(name="keep", bufs=1))
-        ring = ctx.enter_context(tc.tile_pool(name="ring", bufs=2))
-        psum = ctx.enter_context(tc.psum_pool(name="psum", bufs=8))
+        ring = ctx.enter_context(tc.tile_pool(name="ring", bufs=1))
+        psum = ctx.enter_context(tc.psum_pool(name="psum", bufs=1))
 
         def load_list(src, name):
             dst = keep.tile(list(src.shape), U16, name=name)
             nc.sync.dma_start(dst[:], src)
             return dst
+
+        def slot(shape, dtype, tag):
+            return ring.tile(shape, dtype, tag=tag, align_bytes=64, name=tag)
 
         tab_sc = keep.tile([P, T], U8, align_bytes=64)
         nc.vector.memset(tab_sc[:].bitcast(I32), 0)
@@ -51,202 +59,227 @@ def tile_list_village_trap_peaks_kernel(
         for y in y_tiles:
             nc.vector.memset(y[:, V:], 0.0)
 
-        warm = keep.tile([P, 1], F32)
-        nc.scalar.activation(warm[:], y_tiles[0][:, V : V + 1], ACT.Identity)
-
         offs_sb = load_list(offs, "offs_sb")
         tab_w = [keep.tile([P, T], I32, name=f"tab_w{a}") for a in range(k_passes)]
 
         def load_tab(a):
             nc.sync.dma_start(tab_w[a][:], tab_words[a].rearrange("p n i -> p (n i)").bitcast(I32))
 
-        def load_w1(a, c0, width):
-            raw = ring.tile([P, PACK, width], F32, tag="raw", bufs=5, name="raw")
+        def load_w1(a, c0, width, tag, bufs):
+            raw = ring.tile([P, PACK, width], F32, tag=tag, bufs=bufs, name="raw")
             rows = w1[a * KP : (a + 1) * KP, c0 : c0 + width]
             nc.sync.dma_start(raw[:], rows.rearrange("(p j) c -> p j c", j=PACK))
             return raw
 
+        def load_columns(vec, name):
+            dst = keep.tile([P, vec.shape[0] // P], F32, name=name)
+            with nc.allow_non_contiguous_dma(reason="one value a partition and tile"):
+                nc.sync.dma_start(dst[:], vec.rearrange("(c p) -> p c", p=P))
+            return dst
+
         load_tab(0)
-        raw00 = load_w1(0, 0, KP)
-        sc_in = keep.tile([P, T // 4], I32)
-        for q in range(4):
-            live = slice(32 * q, 32 * q + 4 * k_passes)
-            nc.sync.dma_start(sc_in[live, :], tab_scales[:, 4 * q : 4 * q + 4, :].bitcast(I32))
-            nc.vector.tensor_copy(tab_sc[live, :].bitcast(I32), sc_in[live, :])
         load_tab(1)
-        raw01 = load_w1(1, 0, KP)
+        for q in range(4):
+            nc.sync.dma_start(
+                tab_sc[32 * q : 32 * q + 4 * k_passes, :].bitcast(I32),
+                tab_scales[:, 4 * q : 4 * q + 4, :].bitcast(I32),
+            )
+        raw_a = [load_w1(a, 0, PAIR, "narrow", 4) for a in range(k_passes)]
         load_tab(2)
-        b1_sb = [ring.tile([P, PACK], F32, tag=f"woven{1 - b}", bufs=1, align_bytes=64, name="b1_sb") for b in range(r_passes)]
-
-        def load_b1(b):
-            nc.sync.dma_start(b1_sb[b][:], b1[b * KP : (b + 1) * KP].rearrange("(p t) -> p t", t=PACK))
-
-        load_b1(0)
-        raw02 = [load_w1(2, i * 256, 256) for i in range(2)]
+        b1_a = load_columns(b1[0:PAIR], "b1_a")
         pos1_sb = load_list(pos1, "pos1_sb")
         pos2_sb = load_list(pos2, "pos2_sb")
-
-        v_w = [keep.tile([P, S], U32, name=f"v_w{a}", align_bytes=64) for a in range(k_passes)]
-        v_sc = keep.tile([P, S], U8, align_bytes=64)
-        for a in range(k_passes):
-            nc.vector.tensor_copy(v_w[a][:], tab_w[a][:].bitcast(U32).indirect(offs_sb[:]))
-            if a == 0:
-                nc.vector.tensor_copy(v_sc[:], tab_sc[:].indirect(offs_sb[:]))
-
-        def weave_w1(copy, dealt, raw, m0):
-            width = raw.shape[2]
-            dst = dealt[:].rearrange("p (t m j) -> p m j t", t=PACK, j=PACK)
-            copy(dst[:, m0 : m0 + width // PACK], raw.rearrange("p j (m t) -> p m j t", t=PACK))
-
-        def new_dealt(b, a):
-            return ring.tile([P, PACK * KP], BF16, tag=f"dealt{a}", bufs=1, align_bytes=64, name="dealt")
-
-        def quantise(src, cols, name, cuts=None):
-            codes = keep.tile([P, cols], U32, name=name + "_c", align_bytes=64)
-            scales = keep.tile([P, cols], U8, name=name + "_s", align_bytes=64)
-            cuts = cuts or (0, cols)
-            for c0, c1 in zip(cuts, cuts[1:]):
-                nc.vector.quantize_mx(
-                    out=codes[:, c0:c1].bitcast(FP8X4), scales=scales[:, c0:c1], in_=src[:, PACK * c0 : PACK * c1]
-                )
-            return codes, scales
-
-        def first_stage(acc, wq):
-            for t in range(PACK):
-                for a, n in itertools.product(range(k_passes), range(halves)):
-                    codes, scales = wq[a]
-                    cols = slice(n * BANK, (n + 1) * BANK)
-                    nc.tensor.matmul_mx(
-                        out=acc[t][n][:],
-                        lhsT=codes[:, t * P : (t + 1) * P].bitcast(FP8X4),
-                        lhsT_scale=scales[:, t * P : (t + 1) * P],
-                        rhs=v_w[a][:, cols].bitcast(FP8X4),
-                        rhs_scale=v_sc[4 * a : P, cols],
-                        start=(a == 0),
-                        stop=(a == k_passes - 1),
-                    )
-
-        def new_acc():
-            return [[psum.tile([P, BANK], F32, tag="acc", name="acc") for n in range(halves)] for t in range(PACK)]
-
-        h_rows = [keep.tile([P, S], F32, name=f"h_rows{c}") for c in range(H // P)]
-
-        def leave_psum(acc, b, t):
-            h = ring.tile([P, S], F32, tag="h", bufs=6, name="h")
-            bias = b1_sb[b][:, t : t + 1]
-            for n in range(halves):
-                dst = h[:, n * BANK : (n + 1) * BANK]
-                if b == 0 and t == 0:
-                    nc.vector.tensor_scalar(dst, acc[t][n][:], bias, None, ALU.add)
-                else:
-                    nc.scalar.activation(dst, acc[t][n][:], ACT.Identity, bias=bias)
-            for u in range(PACK):
-                nc.sync.dma_start(h_rows[PACK * b + u][t:P:PACK, :], h[32 * u : 32 * (u + 1), :])
-            return h
-
-        def pick(h_pair, x_planes, t0, m0, m1, second_tag, first_tag=None):
-            width = m1 - m0
-            entries = slice(m0 // 16, m1 // 16)
-            if first_tag is None:
-                first = ring.tile([P, 2, width], F32, tag="first", name="first")
-            else:
-                first = ring.tile([P, 2, width], F32, tag=first_tag, bufs=1, align_bytes=64, name="first")
-            if second_tag is None:
-                second = ring.tile([P, 2, width], F32, tag="second", name="second")
-            else:
-                second = ring.tile([P, 2, width], F32, tag=second_tag, bufs=1, align_bytes=64, name="second")
-            for i in range(2):
-                nc.vector.tensor_copy(first[:, i, :], h_pair[i][:].indirect(pos1_sb[:, entries]))
-                nc.vector.tensor_copy(second[:, i, :], h_pair[i][:].indirect(pos2_sb[:, entries]))
-            nc.vector.tensor_tensor(x_planes[:, t0 : t0 + 2, m0:m1], first[:], second[:], ALU.max)
-
-        def weave_x(copy, woven, x_planes, m0, m1):
-            dst = woven[:, PACK * m0 : PACK * m1].rearrange("p (c i t) -> p c t i", i=4, t=PACK)
-            copy(dst, x_planes[:, :, m0:m1].rearrange("p t (c i) -> p c t i", i=4))
-
-        acc0 = new_acc()
-        dealt = new_dealt(0, 0)
-        weave_w1(nc.scalar.copy, dealt, raw00[:], 0)
-        wq0 = [quantise(dealt, KP, "w00")]
-        dealt = new_dealt(0, 1)
-        weave_w1(nc.scalar.copy, dealt, raw01[:], 0)
-        wq0.append(quantise(dealt, KP, "w01"))
-        dealt = new_dealt(0, 2)
-        weave_w1(nc.scalar.copy, dealt, raw02[0][:], 0)
-        weave_w1(nc.scalar.copy, dealt, raw02[1][:], 64)
-        wq0.append(quantise(dealt, KP, "w02", (0, 128, 256, 512)))
-        first_stage(acc0, wq0)
-
-        raw1 = [load_w1(a, KP, KP) for a in range(k_passes)]
-        w4_w = [keep.tile([P, 2 * H], U8, name=f"w4_w{a}", align_bytes=64) for a in range(r_passes)]
-        for a in range(r_passes):
-            nc.sync.dma_start(w4_w[a][:].bitcast(I32), w4_words[a].bitcast(I32))
+        raw_b = [load_w1(0, PAIR, PAIR, "h0", 1), load_w1(1, PAIR, PAIR, "narrow", 4), load_w1(2, PAIR, PAIR, "h1", 1)]
+        b1_b = load_columns(b1[PAIR:KP], "b1_b")
+        raw_c = [load_w1(a, KP, KP, tag, 1) for a, tag in enumerate(("h2", "first4", "second4"))]
+        b1_c = keep.tile([P, PACK], F32)
+        nc.sync.dma_start(b1_c[:], b1[KP:H].rearrange("(p t) -> p t", t=PACK))
+        w4_w = keep.tile([P, r_passes, 2 * H], U8, align_bytes=64)
+        nc.sync.dma_start(w4_w[:].bitcast(I32), w4_words.bitcast(I32).rearrange("a p n -> p a n"))
         for q in range(4):
             nc.sync.dma_start(
                 w4_sc[32 * q : 32 * q + 4, :].bitcast(I32).rearrange("p (a n) -> p a n", a=r_passes),
                 w4_scales[:, 4 * q : 4 * q + 4, :].bitcast(I32).rearrange("a r n -> r a n"),
             )
-        load_b1(1)
         pos3_sb = load_list(pos3, "pos3_sb")
-        gain_sb = keep.tile([P, H // P], F32)
-        with nc.allow_non_contiguous_dma(reason="one gain value a partition and tile"):
-            nc.sync.dma_start(gain_sb[:], gain.rearrange("(c p) -> p c", p=P))
+        gain_sb = load_columns(gain, "gain_sb")
 
-        x_planes = [ring.tile([P, PACK, V], BF16, tag="x_planes", name="x_planes") for b in range(r_passes)]
-        h0 = [leave_psum(acc0, 0, t) for t in range(PACK)]
-        pick(h0[0:2], x_planes[0], 0, 0, V, None)
-        wq1 = []
-        for a in range(k_passes):
-            dealt = new_dealt(1, a)
-            weave_w1(nc.scalar.copy, dealt, raw1[a][:], 0)
-            wq1.append(quantise(dealt, KP, f"w1{a}"))
-        acc1 = new_acc()
-        first_stage(acc1, wq1)
-        pick(h0[2:4], x_planes[0], 2, 0, V, "dealt2", "dealt1")
+        v_w = [keep.tile([P, S], U32, name=f"v_w{a}", align_bytes=64) for a in range(k_passes)]
+        v_sc = keep.tile([P, S], U8, align_bytes=64)
+        for a in range(k_passes - 1):
+            nc.vector.tensor_copy(v_w[a][:], tab_w[a][:].bitcast(U32).indirect(offs_sb[:]))
+        nc.vector.tensor_copy(v_sc[:], tab_sc[:].indirect(offs_sb[:]))
+        for n in range(halves):
+            entries = offs_sb[:, n * BANK // 16 : (n + 1) * BANK // 16]
+            nc.vector.tensor_copy(v_w[-1][:, n * BANK : (n + 1) * BANK], tab_w[-1][:].bitcast(U32).indirect(entries))
 
-        h1 = [leave_psum(acc1, 1, t) for t in range(PACK)]
-        pick(h1[0:2], x_planes[1], 0, 0, V, None)
-        woven0 = ring.tile([P, PACK * V], BF16, tag="woven0", bufs=1, align_bytes=64)
-        weave_x(nc.scalar.copy, woven0, x_planes[0], 0, V)
-        xq = [quantise(woven0, V, "x0")]
+        def weave(woven, planes):
+            dst = woven.rearrange("p (c i t) -> p c t i", i=4, t=PACK)
+            nc.scalar.activation(dst, planes.rearrange("p t (c i) -> p c t i", i=4), ACT.Identity)
 
-        woven1 = ring.tile([P, PACK * V], BF16, tag="woven1", bufs=1, align_bytes=64)
-        x1_c = keep.tile([P, V], U32, align_bytes=64)
-        x1_s = keep.tile([P, V], U8, align_bytes=64)
-        half = V // 2
-        for i, copy in enumerate((nc.scalar.copy, nc.vector.tensor_copy)):
-            m0, m1 = i * half, (i + 1) * half
-            pick(h1[2:4], x_planes[1], 2, m0, m1, "woven0" if i == 0 else None)
-            weave_x(copy, woven1, x_planes[1], m0, m1)
-            nc.vector.quantize_mx(
-                out=x1_c[:, m0:m1].bitcast(FP8X4), scales=x1_s[:, m0:m1], in_=woven1[:, PACK * m0 : PACK * m1]
+        def quantise(src, codes, scales):
+            nc.vector.quantize_mx(out=codes.bitcast(FP8X4), scales=scales, in_=src)
+
+        def quantise_w1(woven, name):
+            cols = woven.shape[1] // PACK
+            codes = keep.tile([P, cols], U32, name=name + "_c", align_bytes=64)
+            scales = keep.tile([P, cols], U8, name=name + "_s", align_bytes=64)
+            quantise(woven[:], codes[:], scales[:])
+            return codes, scales
+
+        def w1_in_row_order(raw, name):
+            woven = slot([P, PACK * PAIR], BF16, name)
+            weave(woven[:], raw[:])
+            return quantise_w1(woven, name)
+
+        def w1_dealt(raw, name):
+            woven = slot([P, PACK * KP], BF16, name)
+            nc.scalar.copy(
+                woven[:].rearrange("p (t m j) -> p m j t", t=PACK, j=PACK),
+                raw[:].rearrange("p j (m t) -> p m j t", t=PACK),
             )
-        xq.append((x1_c, x1_s))
+            return quantise_w1(woven, name)
 
-        acc2 = [psum.tile([P, BANK], F32, tag="acc", name="acc") for c in range(H // P)]
-        for a in range(r_passes):
-            codes, scales = xq[a]
-            for c in range(H // P):
+        def first_stage(wq, i):
+            acc = [psum.tile([P, BANK], F32, tag="acc", bufs=6, name="acc") for n in range(halves)]
+            for a, n in itertools.product(range(k_passes), range(halves)):
+                codes, scales = wq[a]
+                cols = slice(n * BANK, (n + 1) * BANK)
                 nc.tensor.matmul_mx(
-                    out=acc2[c][:],
-                    lhsT=w4_w[a][:, 2 * P * c : 2 * P * (c + 1)].bitcast(FP4X4),
-                    lhsT_scale=w4_sc[:, a * H + c * P : a * H + (c + 1) * P],
-                    rhs=codes[:].bitcast(FP8X4),
-                    rhs_scale=scales[:],
+                    out=acc[n][:],
+                    lhsT=codes[:, i * P : (i + 1) * P].bitcast(FP8X4),
+                    lhsT_scale=scales[:, i * P : (i + 1) * P],
+                    rhs=v_w[a][:, cols].bitcast(FP8X4),
+                    rhs_scale=v_sc[4 * a : P, cols],
                     start=(a == 0),
-                    stop=(a == r_passes - 1),
+                    stop=(a == k_passes - 1),
                 )
+            return acc
 
-        for c in range(H // P):
+        def leave_psum(acc, h, bias, shared):
+            for n in range(halves):
+                dst = h[:, n * BANK : (n + 1) * BANK]
+                if shared and n == halves - 1:
+                    nc.vector.tensor_scalar(dst, acc[n][:], bias, None, ALU.add)
+                else:
+                    nc.scalar.activation(dst, acc[n][:], ACT.Identity, bias=bias)
+
+        def pick(dst, h, pos, m0, m1):
+            nc.vector.tensor_copy(dst, h[:].indirect(pos[:, m0 // 16 : m1 // 16]))
+
+        h_rows = [ring.tile([P, S], F32, tag=f"h{c}", name="h_rows") for c in range(tiles)]
+        x0_planes = keep.tile([P, PACK, V], BF16)
+
+        def village_rows(c, first_tag, second_tag, x_tag):
+            first = slot([P, V], F32, first_tag)
+            second = slot([P, V], F32, second_tag)
+            pick(first[:], h_rows[c], pos1_sb, 0, V)
+            pick(second[:], h_rows[c], pos2_sb, 0, V)
+            x = slot([P, V], BF16, x_tag)
+            nc.vector.tensor_tensor(x[:], first[:], second[:], ALU.max)
+            for t in range(PACK):
+                nc.sync.dma_start(x0_planes[32 * c : 32 * (c + 1), t, :], x[t:P:PACK, :])
+
+        wq_a = [w1_in_row_order(raw_a[a], f"wa{a}") for a in range(k_passes)]
+        acc = [first_stage(wq_a, i) for i in range(2)]
+        wq_b = [w1_in_row_order(raw_b[0], "wb0")]
+        leave_psum(acc[0], h_rows[0], b1_a[:, 0:1], shared=True)
+        wq_b.extend(w1_in_row_order(raw_b[a], f"wb{a}") for a in range(1, k_passes))
+        leave_psum(acc[1], h_rows[1], b1_a[:, 1:2], shared=False)
+        wq_c = [w1_dealt(raw_c[0], "wc0")]
+        for i in range(2):
+            leave_psum(first_stage(wq_b, i), h_rows[2 + i], b1_b[:, i : i + 1], shared=False)
+        wq_c.extend(w1_dealt(raw_c[a], f"wc{a}") for a in range(1, k_passes))
+        village_rows(0, "first", "wb1", "wb2")
+        village_rows(1, "first", "wb1", "wc0")
+        village_rows(2, "first", "wb1", "wc1")
+        village_rows(3, "first", "wc2", "x3")
+
+        h_dealt = [keep.tile([P, S], F32, name=f"h_dealt{t}") for t in range(PACK)]
+        for t in range(PACK):
+            leave_psum(first_stage(wq_c, t), h_dealt[t], b1_c[:, t : t + 1], shared=False)
+            for u in range(PACK):
+                nc.sync.dma_start(h_rows[PACK + u][t:P:PACK, :], h_dealt[t][32 * u : 32 * (u + 1), :])
+
+        x_c = [keep.tile([P, V], U32, name=f"x_c{a}", align_bytes=64) for a in range(r_passes)]
+        x_s = [keep.tile([P, V], U8, name=f"x_s{a}", align_bytes=64) for a in range(r_passes)]
+        woven0 = slot([P, PACK * V], BF16, "woven0")
+        weave(woven0[:], x0_planes[:])
+        quantise(woven0[:], x_c[0][:], x_s[0][:])
+
+        first = ring.tile([P, PACK, V], F32, tag="first4", name="first")
+        second = ring.tile([P, PACK, V], F32, tag="second4", name="second")
+        for t in range(2):
+            pick(first[:, t, :], h_dealt[t], pos1_sb, 0, V)
+            pick(second[:, t, :], h_dealt[t], pos2_sb, 0, V)
+        for t in range(2, PACK):
+            pick(first[:, t, LATE:], h_dealt[t], pos1_sb, 0, EARLY)
+            pick(second[:, t, LATE:], h_dealt[t], pos2_sb, 0, EARLY)
+        early_planes = slot([P, PACK, EARLY], BF16, "woven0")
+        nc.vector.tensor_tensor(early_planes[:, :2, :], first[:, :2, :EARLY], second[:, :2, :EARLY], ALU.max)
+        nc.vector.tensor_tensor(early_planes[:, 2:, :], first[:, 2:, LATE:], second[:, 2:, LATE:], ALU.max)
+        early = keep.tile([P, PACK * EARLY], BF16, align_bytes=64)
+        weave(early[:], early_planes[:])
+        for t in range(2, PACK):
+            pick(first[:, t, EARLY:], h_dealt[t], pos1_sb, EARLY, V)
+            pick(second[:, t, EARLY:], h_dealt[t], pos2_sb, EARLY, V)
+        late = keep.tile([P, PACK * LATE], BF16, align_bytes=64)
+        nc.vector.tensor_tensor(
+            late[:].rearrange("p (c i t) -> p c t i", i=2, t=PACK),
+            first[:, :, EARLY:].rearrange("p t (c i) -> p c t i", i=2),
+            second[:, :, EARLY:].rearrange("p t (c i) -> p c t i", i=2),
+            ALU.max,
+        )
+        quantise(late[:], x_c[1][:, EARLY:], x_s[1][:, EARLY:])
+        for m0, m1 in ((0, PAIR), (PAIR, EARLY)):
+            quantise(early[:, PACK * m0 : PACK * m1], x_c[1][:, m0:m1], x_s[1][:, m0:m1])
+
+        def second_pass(acc, c, a, m0, m1, start, stop):
+            nc.tensor.matmul_mx(
+                out=acc[:, m0:m1],
+                lhsT=w4_w[:, a, 2 * P * c : 2 * P * (c + 1)].bitcast(FP4X4),
+                lhsT_scale=w4_sc[:, a * H + c * P : a * H + (c + 1) * P],
+                rhs=x_c[a][:, m0:m1].bitcast(FP8X4),
+                rhs_scale=x_s[a][:, m0:m1],
+                start=start,
+                stop=stop,
+            )
+
+        def scores(c):
+            if c < 2:
+                acc = psum.tile([P, BANK], F32, tag="spare", bufs=2, name="acc")
+            else:
+                acc = psum.tile([P, BANK], F32, tag="acc", bufs=6, name="acc")
+            second_pass(acc, c, 0, 0, V, True, False)
+            if c == 0:
+                starts = [EARLY] + list(range(0, EARLY, LATE))
+                for m0 in starts:
+                    second_pass(acc, c, 1, m0, m0 + LATE, False, m0 == starts[-1])
+            else:
+                second_pass(acc, c, 1, 0, V, False, True)
+            return acc
+
+        acc2 = [scores(c) for c in range(tiles)]
+
+        def spread(c, j0, j1):
             y = y_tiles[c % Y_TILES]
-            nc.scalar.copy(y[:, :V], acc2[c][:])
-            pieces = 2 if c == H // P - 1 else 1
-            width = S // pieces
-            for i in range(pieces):
-                cols = slice(i * width, (i + 1) * width)
-                up = ring.tile([P, width], F32, tag="up", bufs=3, name="up")
-                nc.vector.tensor_copy(up[:], y[:].indirect(pos3_sb[:, i * width // 16 : (i + 1) * width // 16]))
-                nc.vector.scalar_tensor_tensor(
-                    up[:], h_rows[c][:, cols], gain_sb[:, c : c + 1], up[:], ALU.mult, ALU.max
-                )
-                nc.sync.dma_start(out[c * P : (c + 1) * P, cols], up[:])
+            if j0 == 0:
+                nc.scalar.copy(y[:, :V], acc2[c][:])
+            up = ring.tile([P, j1 - j0], F32, tag="narrow", bufs=4, name="up")
+            pick(up[:], y, pos3_sb, j0, j1)
+            return up
+
+        def finish(up, c, j0, j1):
+            nc.vector.scalar_tensor_tensor(
+                up[:], h_rows[c][:, j0:j1], gain_sb[:, c : c + 1], up[:], ALU.mult, ALU.max
+            )
+            nc.sync.dma_start(out[c * P : (c + 1) * P, j0:j1], up[:])
+
+        pieces = [(c, 0, S) for c in range(tiles - 1)]
+        pieces.extend((tiles - 1, j0, j1) for j0, j1 in zip(LAST_CUTS, LAST_CUTS[1:]))
+        ahead = spread(*pieces[0])
+        for piece, following in zip(pieces, pieces[1:] + [None]):
+            up = ahead
+            if following is not None:
+                ahead = spread(*following)
+            finish(up, *piece)

@@ -2,6 +2,7 @@ import itertools
 from contextlib import ExitStack
 
 import concourse.mybir as mybir
+from concourse.masks import make_identity
 
 K, H, T, S, V = 1536, 1024, 2048, 1024, 512
 FLOPS = 2 * K * H * S + 2 * H * H * V
@@ -26,6 +27,7 @@ Y_WINDOW = 1408
 Y_TILES = 3
 LATE = 128
 EARLY = V - LATE
+UP_BUFS = 6
 LAST_CUTS = (0, 512, 768, 1024)
 
 
@@ -53,6 +55,10 @@ def tile_list_village_trap_peaks_kernel(
 
         tab_sc = keep.tile([P, T], U8, align_bytes=64)
         nc.vector.memset(tab_sc[:].bitcast(I32), 0)
+        vec_rows = keep.tile([P, P], F32)
+        nc.vector.memset(vec_rows[:], 0.0)
+        identity = keep.tile([P, P], F32)
+        make_identity(nc, identity[:])
         w4_sc = keep.tile([P, r_passes * H], U8, align_bytes=64)
         nc.vector.memset(w4_sc[:].bitcast(I32), 0)
         y_tiles = [keep.tile([P, Y_WINDOW], F32, name=f"y{i}") for i in range(Y_TILES)]
@@ -71,12 +77,6 @@ def tile_list_village_trap_peaks_kernel(
             nc.sync.dma_start(raw[:], rows.rearrange("(p j) c -> p j c", j=PACK))
             return raw
 
-        def load_columns(vec, name):
-            dst = keep.tile([P, vec.shape[0] // P], F32, name=name)
-            with nc.allow_non_contiguous_dma(reason="one value a partition and tile"):
-                nc.sync.dma_start(dst[:], vec.rearrange("(c p) -> p c", p=P))
-            return dst
-
         load_tab(0)
         load_tab(1)
         for q in range(4):
@@ -84,14 +84,14 @@ def tile_list_village_trap_peaks_kernel(
                 tab_sc[32 * q : 32 * q + 4 * k_passes, :].bitcast(I32),
                 tab_scales[:, 4 * q : 4 * q + 4, :].bitcast(I32),
             )
-        raw_a = [load_w1(a, 0, PAIR, "narrow", 4) for a in range(k_passes)]
+        nc.sync.dma_start(vec_rows[:PACK, :], b1[:KP].rearrange("(c p) -> c p", p=P))
+        nc.sync.dma_start(vec_rows[PACK : PACK + tiles, :], gain.rearrange("(c p) -> c p", p=P))
+        raw_a = [load_w1(a, 0, PAIR, "narrow", UP_BUFS) for a in range(k_passes)]
         load_tab(2)
-        b1_a = load_columns(b1[0:PAIR], "b1_a")
         pos1_sb = load_list(pos1, "pos1_sb")
         pos2_sb = load_list(pos2, "pos2_sb")
-        raw_b = [load_w1(0, PAIR, PAIR, "h0", 1), load_w1(1, PAIR, PAIR, "narrow", 4), load_w1(2, PAIR, PAIR, "h1", 1)]
-        b1_b = load_columns(b1[PAIR:KP], "b1_b")
-        raw_c = [load_w1(a, KP, KP, tag, 1) for a, tag in enumerate(("h2", "first4", "second4"))]
+        raw_b = [load_w1(0, PAIR, PAIR, "b0", 1), load_w1(1, PAIR, PAIR, "b1", 1), load_w1(2, PAIR, PAIR, "b2", 1)]
+        raw_c = [load_w1(a, KP, KP, tag, 1) for a, tag in enumerate(("c0", "c1", "c2"))]
         b1_c = keep.tile([P, PACK], F32)
         nc.sync.dma_start(b1_c[:], b1[KP:H].rearrange("(p t) -> p t", t=PACK))
         w4_w = keep.tile([P, r_passes, 2 * H], U8, align_bytes=64)
@@ -102,7 +102,11 @@ def tile_list_village_trap_peaks_kernel(
                 w4_scales[:, 4 * q : 4 * q + 4, :].bitcast(I32).rearrange("a r n -> r a n"),
             )
         pos3_sb = load_list(pos3, "pos3_sb")
-        gain_sb = load_columns(gain, "gain_sb")
+
+        turned = psum.tile([P, P], F32, tag="spare", bufs=2)
+        nc.tensor.transpose(turned[:], vec_rows[:], identity[:])
+        vec_cols = keep.tile([P, PACK + tiles], F32)
+        nc.scalar.copy(vec_cols[:], turned[:, : PACK + tiles])
 
         v_w = [keep.tile([P, S], U32, name=f"v_w{a}", align_bytes=64) for a in range(k_passes)]
         v_sc = keep.tile([P, S], U8, align_bytes=64)
@@ -127,8 +131,8 @@ def tile_list_village_trap_peaks_kernel(
             quantise(woven[:], codes[:], scales[:])
             return codes, scales
 
-        def w1_in_row_order(raw, name):
-            woven = slot([P, PACK * PAIR], BF16, name)
+        def w1_in_row_order(raw, name, tag):
+            woven = slot([P, PACK * PAIR], BF16, tag)
             weave(woven[:], raw[:])
             return quantise_w1(woven, name)
 
@@ -156,122 +160,138 @@ def tile_list_village_trap_peaks_kernel(
                 )
             return acc
 
-        def leave_psum(acc, h, bias, shared):
+        def leave_psum(acc, h, bias, on_vector=False):
             for n in range(halves):
                 dst = h[:, n * BANK : (n + 1) * BANK]
-                if shared and n == halves - 1:
+                if on_vector:
                     nc.vector.tensor_scalar(dst, acc[n][:], bias, None, ALU.add)
                 else:
                     nc.scalar.activation(dst, acc[n][:], ACT.Identity, bias=bias)
 
         def pick(dst, h, pos, m0, m1):
-            nc.vector.tensor_copy(dst, h[:].indirect(pos[:, m0 // 16 : m1 // 16]))
+            nc.vector.tensor_copy(dst, h.indirect(pos[:, m0 // 16 : m1 // 16]))
 
-        h_rows = [ring.tile([P, S], F32, tag=f"h{c}", name="h_rows") for c in range(tiles)]
-        x0_planes = keep.tile([P, PACK, V], BF16)
+        def after(tag, width, dtype):
+            return ring.tile([P, width], dtype, tag=tag, name=tag)
 
-        def village_rows(c, first_tag, second_tag, x_tag):
-            first = slot([P, V], F32, first_tag)
-            second = slot([P, V], F32, second_tag)
-            pick(first[:], h_rows[c], pos1_sb, 0, V)
-            pick(second[:], h_rows[c], pos2_sb, 0, V)
-            x = slot([P, V], BF16, x_tag)
-            nc.vector.tensor_tensor(x[:], first[:], second[:], ALU.max)
+        after_b0 = after("b0", S + 2 * V, F32)
+        after_b2 = after("b2", 2 * V, F32)
+        own = [keep.tile([P, S], F32, name=f"h_rows{c}") for c in (0, 2)]
+        h_rows = [own[0][:], after_b0[:, :S], own[1][:], after("c2", S, F32)[:]]
+        x_last = keep.tile([P, V], BF16)
+        x0_planes = slot([P, PACK, V], BF16, "planes")
+
+        def village_rows(c, first, second, x):
+            pick(first, h_rows[c], pos1_sb, 0, V)
+            pick(second, h_rows[c], pos2_sb, 0, V)
+            nc.vector.tensor_tensor(x, first, second, ALU.max)
             for t in range(PACK):
                 nc.sync.dma_start(x0_planes[32 * c : 32 * (c + 1), t, :], x[t:P:PACK, :])
 
-        wq_a = [w1_in_row_order(raw_a[a], f"wa{a}") for a in range(k_passes)]
+        wq_a = [w1_in_row_order(raw_a[a], f"wa{a}", f"woven{a}") for a in range(k_passes)]
         acc = [first_stage(wq_a, i) for i in range(2)]
-        wq_b = [w1_in_row_order(raw_b[0], "wb0")]
-        leave_psum(acc[0], h_rows[0], b1_a[:, 0:1], shared=True)
-        wq_b.extend(w1_in_row_order(raw_b[a], f"wb{a}") for a in range(1, k_passes))
-        leave_psum(acc[1], h_rows[1], b1_a[:, 1:2], shared=False)
+        leave_psum(acc[0], h_rows[0], vec_cols[:, 0:1], on_vector=True)
+        wq_b = [w1_in_row_order(raw_b[0], "wb0", "woven0")]
+        leave_psum(acc[1], h_rows[1], vec_cols[:, 1:2])
+        wq_b.extend(w1_in_row_order(raw_b[a], f"wb{a}", f"woven{a}") for a in range(1, k_passes))
         wq_c = [w1_dealt(raw_c[0], "wc0")]
-        for i in range(2):
-            leave_psum(first_stage(wq_b, i), h_rows[2 + i], b1_b[:, i : i + 1], shared=False)
+        leave_psum(first_stage(wq_b, 0), h_rows[2], vec_cols[:, 2:3])
+        acc = first_stage(wq_b, 1)
         wq_c.extend(w1_dealt(raw_c[a], f"wc{a}") for a in range(1, k_passes))
-        village_rows(0, "first", "wb1", "wb2")
-        village_rows(1, "first", "wb1", "wc0")
-        village_rows(2, "first", "wb1", "wc1")
-        village_rows(3, "first", "wc2", "x3")
+        leave_psum(acc, h_rows[3], vec_cols[:, 3:4])
+        even = after_b0[:, S : S + V], after_b0[:, S + V :]
+        odd = after_b2[:, :V], after_b2[:, V:]
+        village_rows(0, *even, after("b1", V, BF16)[:])
+        village_rows(1, *odd, after("c0", V, BF16)[:])
+        village_rows(2, *even, after("c1", V, BF16)[:])
+        village_rows(3, *odd, x_last[:])
 
         h_dealt = [keep.tile([P, S], F32, name=f"h_dealt{t}") for t in range(PACK)]
         for t in range(PACK):
-            leave_psum(first_stage(wq_c, t), h_dealt[t], b1_c[:, t : t + 1], shared=False)
-            for u in range(PACK):
-                nc.sync.dma_start(h_rows[PACK + u][t:P:PACK, :], h_dealt[t][32 * u : 32 * (u + 1), :])
+            leave_psum(first_stage(wq_c, t), h_dealt[t][:], b1_c[:, t : t + 1])
 
         x_c = [keep.tile([P, V], U32, name=f"x_c{a}", align_bytes=64) for a in range(r_passes)]
         x_s = [keep.tile([P, V], U8, name=f"x_s{a}", align_bytes=64) for a in range(r_passes)]
-        woven0 = slot([P, PACK * V], BF16, "woven0")
-        weave(woven0[:], x0_planes[:])
-        quantise(woven0[:], x_c[0][:], x_s[0][:])
+        x0_woven = slot([P, PACK * V], BF16, "x0_woven")
+        weave(x0_woven[:], x0_planes[:])
 
-        first = ring.tile([P, PACK, V], F32, tag="first4", name="first")
-        second = ring.tile([P, PACK, V], F32, tag="second4", name="second")
+        first = keep.tile([P, PACK, V], F32)
+        second = keep.tile([P, PACK, V], F32)
         for t in range(2):
-            pick(first[:, t, :], h_dealt[t], pos1_sb, 0, V)
-            pick(second[:, t, :], h_dealt[t], pos2_sb, 0, V)
+            pick(first[:, t, :], h_dealt[t][:], pos1_sb, 0, V)
+            pick(second[:, t, :], h_dealt[t][:], pos2_sb, 0, V)
         for t in range(2, PACK):
-            pick(first[:, t, LATE:], h_dealt[t], pos1_sb, 0, EARLY)
-            pick(second[:, t, LATE:], h_dealt[t], pos2_sb, 0, EARLY)
-        early_planes = slot([P, PACK, EARLY], BF16, "woven0")
-        nc.vector.tensor_tensor(early_planes[:, :2, :], first[:, :2, :EARLY], second[:, :2, :EARLY], ALU.max)
-        nc.vector.tensor_tensor(early_planes[:, 2:, :], first[:, 2:, LATE:], second[:, 2:, LATE:], ALU.max)
-        early = keep.tile([P, PACK * EARLY], BF16, align_bytes=64)
-        weave(early[:], early_planes[:])
+            pick(first[:, t, LATE:], h_dealt[t][:], pos1_sb, 0, EARLY)
+            pick(second[:, t, LATE:], h_dealt[t][:], pos2_sb, 0, EARLY)
+        quantise(x0_woven[:], x_c[0][:], x_s[0][:])
+        h_moved = slot([P, PACK * S], F32, "x0_woven")
+        for u in range(PACK):
+            h_rows.append(h_moved[:, u * S : (u + 1) * S])
+            for t in range(PACK):
+                nc.sync.dma_start(h_rows[PACK + u][t:P:PACK, :], h_dealt[t][32 * u : 32 * (u + 1), :])
+
+        early_planes = slot([P, PACK * EARLY], BF16, "planes")
+        early = []
+        for m0, m1 in ((0, PAIR), (PAIR, EARLY)):
+            planes = early_planes[:, PACK * m0 : PACK * m1].rearrange("p (t m) -> p t m", t=PACK)
+            shifted = slice(LATE + m0, LATE + m1)
+            nc.vector.tensor_tensor(planes[:, 2:, :], first[:, 2:, shifted], second[:, 2:, shifted], ALU.max)
+            nc.vector.tensor_tensor(planes[:, :2, :], first[:, :2, m0:m1], second[:, :2, m0:m1], ALU.max)
+            woven = keep.tile([P, PACK * (m1 - m0)], BF16, align_bytes=64, name=f"early{m0}")
+            weave(woven[:], planes)
+            early.append(woven)
         for t in range(2, PACK):
-            pick(first[:, t, EARLY:], h_dealt[t], pos1_sb, EARLY, V)
-            pick(second[:, t, EARLY:], h_dealt[t], pos2_sb, EARLY, V)
-        late = keep.tile([P, PACK * LATE], BF16, align_bytes=64)
+            pick(first[:, t, EARLY:], h_dealt[t][:], pos1_sb, EARLY, V)
+            pick(second[:, t, EARLY:], h_dealt[t][:], pos2_sb, EARLY, V)
+        quantise(early[0][:], x_c[1][:, :PAIR], x_s[1][:, :PAIR])
+        late = slot([P, PACK * LATE], BF16, "planes")
         nc.vector.tensor_tensor(
             late[:].rearrange("p (c i t) -> p c t i", i=2, t=PACK),
             first[:, :, EARLY:].rearrange("p t (c i) -> p c t i", i=2),
             second[:, :, EARLY:].rearrange("p t (c i) -> p c t i", i=2),
             ALU.max,
         )
+        quantise(early[1][:], x_c[1][:, PAIR:EARLY], x_s[1][:, PAIR:EARLY])
         quantise(late[:], x_c[1][:, EARLY:], x_s[1][:, EARLY:])
-        for m0, m1 in ((0, PAIR), (PAIR, EARLY)):
-            quantise(early[:, PACK * m0 : PACK * m1], x_c[1][:, m0:m1], x_s[1][:, m0:m1])
 
-        def second_pass(acc, c, a, m0, m1, start, stop):
+        def second_pass(acc, c, a, m0, m1):
             nc.tensor.matmul_mx(
-                out=acc[:, m0:m1],
+                out=acc,
                 lhsT=w4_w[:, a, 2 * P * c : 2 * P * (c + 1)].bitcast(FP4X4),
                 lhsT_scale=w4_sc[:, a * H + c * P : a * H + (c + 1) * P],
                 rhs=x_c[a][:, m0:m1].bitcast(FP8X4),
                 rhs_scale=x_s[a][:, m0:m1],
-                start=start,
-                stop=stop,
+                start=(a == 0),
+                stop=(a == r_passes - 1),
             )
 
-        def scores(c):
-            if c < 2:
-                acc = psum.tile([P, BANK], F32, tag="spare", bufs=2, name="acc")
-            else:
-                acc = psum.tile([P, BANK], F32, tag="acc", bufs=6, name="acc")
-            second_pass(acc, c, 0, 0, V, True, False)
-            if c == 0:
-                starts = [EARLY] + list(range(0, EARLY, LATE))
-                for m0 in starts:
-                    second_pass(acc, c, 1, m0, m0 + LATE, False, m0 == starts[-1])
-            else:
-                second_pass(acc, c, 1, 0, V, False, True)
-            return acc
+        def first_scores(y):
+            for m0, m1, tag, bufs in ((0, PAIR, "acc", 6), (PAIR, EARLY, "spare", 2), (EARLY, V, "spare", 2)):
+                acc = psum.tile([P, m1 - m0], F32, tag=tag, bufs=bufs, name="acc")
+                for m in range(m0, m1, LATE):
+                    for a in range(r_passes):
+                        second_pass(acc[:, m - m0 : m - m0 + LATE], 0, a, m, m + LATE)
+                nc.scalar.copy(y[:, m0:m1], acc[:])
 
-        acc2 = [scores(c) for c in range(tiles)]
+        def scores(c, y):
+            acc = psum.tile([P, V], F32, tag="acc", bufs=6, name="acc")
+            for a in range(r_passes):
+                second_pass(acc[:], c, a, 0, V)
+            nc.scalar.copy(y[:, :V], acc[:])
 
         def spread(c, j0, j1):
             y = y_tiles[c % Y_TILES]
-            if j0 == 0:
-                nc.scalar.copy(y[:, :V], acc2[c][:])
-            up = ring.tile([P, j1 - j0], F32, tag="narrow", bufs=4, name="up")
-            pick(up[:], y, pos3_sb, j0, j1)
+            if c == 0:
+                first_scores(y)
+            elif j0 == 0:
+                scores(c, y)
+            up = ring.tile([P, j1 - j0], F32, tag="narrow", bufs=UP_BUFS, name="up")
+            pick(up[:], y[:], pos3_sb, j0, j1)
             return up
 
         def finish(up, c, j0, j1):
             nc.vector.scalar_tensor_tensor(
-                up[:], h_rows[c][:, j0:j1], gain_sb[:, c : c + 1], up[:], ALU.mult, ALU.max
+                up[:], h_rows[c][:, j0:j1], vec_cols[:, PACK + c : PACK + c + 1], up[:], ALU.mult, ALU.max
             )
             nc.sync.dma_start(out[c * P : (c + 1) * P, j0:j1], up[:])
 

import itertools
from contextlib import ExitStack

import concourse.mybir as mybir
from concourse.masks import make_identity

K, H, T, S, V = 1536, 1024, 2048, 1024, 512
FLOPS = 2 * K * H * S + 2 * H * H * V

F32 = mybir.dt.float32
BF16 = mybir.dt.bfloat16
I32 = mybir.dt.int32
U32 = mybir.dt.uint32
U16 = mybir.dt.uint16
U8 = mybir.dt.uint8
FP8X4 = mybir.dt.float8_e4m3fn_x4
FP4X4 = mybir.dt.float4_e2m1fn_x4
ALU = mybir.AluOpType
ACT = mybir.ActivationFunctionType

P = 128
PACK = 4
KP = P * PACK
BANK = 512
PAIR = 2 * P
Y_WINDOW = 1408
Y_TILES = 3
LATE = 128
EARLY = V - LATE
UP_BUFS = 6
LAST_CUTS = (0, 512, 768, 1024)


def tile_list_village_trap_peaks_kernel(
    tc, tab_words, tab_scales, offs, w1, b1, pos1, pos2, pos3, w4_words, w4_scales, gain, out
):
    nc = tc.nc
    k_passes = K // KP
    r_passes = H // KP
    halves = S // BANK
    tiles = H // P

    with ExitStack() as ctx:
        keep = ctx.enter_context(tc.tile_pool(name="keep", bufs=1))
        ring = ctx.enter_context(tc.tile_pool(name="ring", bufs=1))
        psum = ctx.enter_context(tc.psum_pool(name="psum", bufs=1))

        def load_list(src, name):
            dst = keep.tile(list(src.shape), U16, name=name)
            nc.sync.dma_start(dst[:], src)
            return dst

        def slot(shape, dtype, tag):
            return ring.tile(shape, dtype, tag=tag, align_bytes=64, name=tag)

        tab_sc = keep.tile([P, T], U8, align_bytes=64)
        nc.vector.memset(tab_sc[:].bitcast(I32), 0)
        vec_rows = keep.tile([P, P], F32)
        nc.vector.memset(vec_rows[:], 0.0)
        identity = keep.tile([P, P], F32)
        make_identity(nc, identity[:])
        w4_sc = keep.tile([P, r_passes * H], U8, align_bytes=64)
        nc.vector.memset(w4_sc[:].bitcast(I32), 0)
        y_tiles = [keep.tile([P, Y_WINDOW], F32, name=f"y{i}") for i in range(Y_TILES)]
        for y in y_tiles:
            nc.vector.memset(y[:, V:], 0.0)

        offs_sb = load_list(offs, "offs_sb")
        tab_w = [keep.tile([P, T], I32, name=f"tab_w{a}") for a in range(k_passes)]

        def load_tab(a):
            nc.sync.dma_start(tab_w[a][:], tab_words[a].rearrange("p n i -> p (n i)").bitcast(I32))

        def load_w1(a, c0, width, tag, bufs):
            raw = ring.tile([P, PACK, width], F32, tag=tag, bufs=bufs, name="raw")
            rows = w1[a * KP : (a + 1) * KP, c0 : c0 + width]
            nc.sync.dma_start(raw[:], rows.rearrange("(p j) c -> p j c", j=PACK))
            return raw

        load_tab(0)
        load_tab(1)
        for q in range(4):
            nc.sync.dma_start(
                tab_sc[32 * q : 32 * q + 4 * k_passes, :].bitcast(I32),
                tab_scales[:, 4 * q : 4 * q + 4, :].bitcast(I32),
            )
        nc.sync.dma_start(vec_rows[:PACK, :], b1[:KP].rearrange("(c p) -> c p", p=P))
        nc.sync.dma_start(vec_rows[PACK : PACK + tiles, :], gain.rearrange("(c p) -> c p", p=P))
        raw_a = [load_w1(a, 0, PAIR, "narrow", UP_BUFS) for a in range(k_passes)]
        load_tab(2)
        pos1_sb = load_list(pos1, "pos1_sb")
        pos2_sb = load_list(pos2, "pos2_sb")
        raw_b = [load_w1(0, PAIR, PAIR, "b0", 1), load_w1(1, PAIR, PAIR, "b1", 1), load_w1(2, PAIR, PAIR, "b2", 1)]
        raw_c = [load_w1(a, KP, KP, tag, 1) for a, tag in enumerate(("c0", "c1", "c2"))]
        b1_c = keep.tile([P, PACK], F32)
        nc.sync.dma_start(b1_c[:], b1[KP:H].rearrange("(p t) -> p t", t=PACK))
        w4_w = keep.tile([P, r_passes, 2 * H], U8, align_bytes=64)
        nc.sync.dma_start(w4_w[:].bitcast(I32), w4_words.bitcast(I32).rearrange("a p n -> p a n"))
        for q in range(4):
            nc.sync.dma_start(
                w4_sc[32 * q : 32 * q + 4, :].bitcast(I32).rearrange("p (a n) -> p a n", a=r_passes),
                w4_scales[:, 4 * q : 4 * q + 4, :].bitcast(I32).rearrange("a r n -> r a n"),
            )
        pos3_sb = load_list(pos3, "pos3_sb")

        turned = psum.tile([P, P], F32, tag="spare", bufs=2)
        nc.tensor.transpose(turned[:], vec_rows[:], identity[:])
        vec_cols = keep.tile([P, PACK + tiles], F32)
        nc.scalar.copy(vec_cols[:], turned[:, : PACK + tiles])

        v_w = [keep.tile([P, S], U32, name=f"v_w{a}", align_bytes=64) for a in range(k_passes)]
        v_sc = keep.tile([P, S], U8, align_bytes=64)
        for a in range(k_passes - 1):
            nc.vector.tensor_copy(v_w[a][:], tab_w[a][:].bitcast(U32).indirect(offs_sb[:]))
        nc.vector.tensor_copy(v_sc[:], tab_sc[:].indirect(offs_sb[:]))
        for n in range(halves):
            entries = offs_sb[:, n * BANK // 16 : (n + 1) * BANK // 16]
            nc.vector.tensor_copy(v_w[-1][:, n * BANK : (n + 1) * BANK], tab_w[-1][:].bitcast(U32).indirect(entries))

        def weave(woven, planes):
            dst = woven.rearrange("p (c i t) -> p c t i", i=4, t=PACK)
            nc.scalar.activation(dst, planes.rearrange("p t (c i) -> p c t i", i=4), ACT.Identity)

        def quantise(src, codes, scales):
            nc.vector.quantize_mx(out=codes.bitcast(FP8X4), scales=scales, in_=src)

        def quantise_w1(woven, name):
            cols = woven.shape[1] // PACK
            codes = keep.tile([P, cols], U32, name=name + "_c", align_bytes=64)
            scales = keep.tile([P, cols], U8, name=name + "_s", align_bytes=64)
            quantise(woven[:], codes[:], scales[:])
            return codes, scales

        def w1_in_row_order(raw, name, tag):
            woven = slot([P, PACK * PAIR], BF16, tag)
            weave(woven[:], raw[:])
            return quantise_w1(woven, name)

        def w1_dealt(raw, name):
            woven = slot([P, PACK * KP], BF16, name)
            nc.scalar.copy(
                woven[:].rearrange("p (t m j) -> p m j t", t=PACK, j=PACK),
                raw[:].rearrange("p j (m t) -> p m j t", t=PACK),
            )
            return quantise_w1(woven, name)

        def first_stage(wq, i):
            acc = [psum.tile([P, BANK], F32, tag="acc", bufs=6, name="acc") for n in range(halves)]
            for a, n in itertools.product(range(k_passes), range(halves)):
                codes, scales = wq[a]
                cols = slice(n * BANK, (n + 1) * BANK)
                nc.tensor.matmul_mx(
                    out=acc[n][:],
                    lhsT=codes[:, i * P : (i + 1) * P].bitcast(FP8X4),
                    lhsT_scale=scales[:, i * P : (i + 1) * P],
                    rhs=v_w[a][:, cols].bitcast(FP8X4),
                    rhs_scale=v_sc[4 * a : P, cols],
                    start=(a == 0),
                    stop=(a == k_passes - 1),
                )
            return acc

        def leave_psum(acc, h, bias, on_vector=False):
            for n in range(halves):
                dst = h[:, n * BANK : (n + 1) * BANK]
                if on_vector:
                    nc.vector.tensor_scalar(dst, acc[n][:], bias, None, ALU.add)
                else:
                    nc.scalar.activation(dst, acc[n][:], ACT.Identity, bias=bias)

        def pick(dst, h, pos, m0, m1):
            nc.vector.tensor_copy(dst, h.indirect(pos[:, m0 // 16 : m1 // 16]))

        def after(tag, width, dtype):
            return ring.tile([P, width], dtype, tag=tag, name=tag)

        after_b0 = after("b0", S + 2 * V, F32)
        after_b2 = after("b2", 2 * V, F32)
        own = [keep.tile([P, S], F32, name=f"h_rows{c}") for c in (0, 2)]
        h_rows = [own[0][:], after_b0[:, :S], own[1][:], after("c2", S, F32)[:]]
        x_last = keep.tile([P, V], BF16)
        x0_planes = slot([P, PACK, V], BF16, "planes")

        def village_rows(c, first, second, x):
            pick(first, h_rows[c], pos1_sb, 0, V)
            pick(second, h_rows[c], pos2_sb, 0, V)
            nc.vector.tensor_tensor(x, first, second, ALU.max)
            for t in range(PACK):
                nc.sync.dma_start(x0_planes[32 * c : 32 * (c + 1), t, :], x[t:P:PACK, :])

        wq_a = [w1_in_row_order(raw_a[a], f"wa{a}", f"woven{a}") for a in range(k_passes)]
        acc = [first_stage(wq_a, i) for i in range(2)]
        leave_psum(acc[0], h_rows[0], vec_cols[:, 0:1], on_vector=True)
        wq_b = [w1_in_row_order(raw_b[0], "wb0", "woven0")]
        leave_psum(acc[1], h_rows[1], vec_cols[:, 1:2])
        wq_b.extend(w1_in_row_order(raw_b[a], f"wb{a}", f"woven{a}") for a in range(1, k_passes))
        wq_c = [w1_dealt(raw_c[0], "wc0")]
        leave_psum(first_stage(wq_b, 0), h_rows[2], vec_cols[:, 2:3])
        acc = first_stage(wq_b, 1)
        wq_c.extend(w1_dealt(raw_c[a], f"wc{a}") for a in range(1, k_passes))
        leave_psum(acc, h_rows[3], vec_cols[:, 3:4])
        even = after_b0[:, S : S + V], after_b0[:, S + V :]
        odd = after_b2[:, :V], after_b2[:, V:]
        village_rows(0, *even, after("b1", V, BF16)[:])
        village_rows(1, *odd, after("c0", V, BF16)[:])
        village_rows(2, *even, after("c1", V, BF16)[:])
        village_rows(3, *odd, x_last[:])

        h_dealt = [keep.tile([P, S], F32, name=f"h_dealt{t}") for t in range(PACK)]
        for t in range(PACK):
            leave_psum(first_stage(wq_c, t), h_dealt[t][:], b1_c[:, t : t + 1])

        x_c = [keep.tile([P, V], U32, name=f"x_c{a}", align_bytes=64) for a in range(r_passes)]
        x_s = [keep.tile([P, V], U8, name=f"x_s{a}", align_bytes=64) for a in range(r_passes)]
        x0_woven = slot([P, PACK * V], BF16, "x0_woven")
        weave(x0_woven[:], x0_planes[:])

        first = keep.tile([P, PACK, V], F32)
        second = keep.tile([P, PACK, V], F32)
        for t in range(2):
            pick(first[:, t, :], h_dealt[t][:], pos1_sb, 0, V)
            pick(second[:, t, :], h_dealt[t][:], pos2_sb, 0, V)
        for t in range(2, PACK):
            pick(first[:, t, LATE:], h_dealt[t][:], pos1_sb, 0, EARLY)
            pick(second[:, t, LATE:], h_dealt[t][:], pos2_sb, 0, EARLY)
        quantise(x0_woven[:], x_c[0][:], x_s[0][:])
        h_moved = slot([P, PACK * S], F32, "x0_woven")
        for u in range(PACK):
            h_rows.append(h_moved[:, u * S : (u + 1) * S])
            for t in range(PACK):
                nc.sync.dma_start(h_rows[PACK + u][t:P:PACK, :], h_dealt[t][32 * u : 32 * (u + 1), :])

        early_planes = slot([P, PACK * EARLY], BF16, "planes")
        early = []
        for m0, m1 in ((0, PAIR), (PAIR, EARLY)):
            planes = early_planes[:, PACK * m0 : PACK * m1].rearrange("p (t m) -> p t m", t=PACK)
            shifted = slice(LATE + m0, LATE + m1)
            nc.vector.tensor_tensor(planes[:, 2:, :], first[:, 2:, shifted], second[:, 2:, shifted], ALU.max)
            nc.vector.tensor_tensor(planes[:, :2, :], first[:, :2, m0:m1], second[:, :2, m0:m1], ALU.max)
            woven = keep.tile([P, PACK * (m1 - m0)], BF16, align_bytes=64, name=f"early{m0}")
            weave(woven[:], planes)
            early.append(woven)
        for t in range(2, PACK):
            pick(first[:, t, EARLY:], h_dealt[t][:], pos1_sb, EARLY, V)
            pick(second[:, t, EARLY:], h_dealt[t][:], pos2_sb, EARLY, V)
        quantise(early[0][:], x_c[1][:, :PAIR], x_s[1][:, :PAIR])
        late = slot([P, PACK * LATE], BF16, "planes")
        nc.vector.tensor_tensor(
            late[:].rearrange("p (c i t) -> p c t i", i=2, t=PACK),
            first[:, :, EARLY:].rearrange("p t (c i) -> p c t i", i=2),
            second[:, :, EARLY:].rearrange("p t (c i) -> p c t i", i=2),
            ALU.max,
        )
        quantise(early[1][:], x_c[1][:, PAIR:EARLY], x_s[1][:, PAIR:EARLY])
        quantise(late[:], x_c[1][:, EARLY:], x_s[1][:, EARLY:])

        def second_pass(acc, c, a, m0, m1):
            nc.tensor.matmul_mx(
                out=acc,
                lhsT=w4_w[:, a, 2 * P * c : 2 * P * (c + 1)].bitcast(FP4X4),
                lhsT_scale=w4_sc[:, a * H + c * P : a * H + (c + 1) * P],
                rhs=x_c[a][:, m0:m1].bitcast(FP8X4),
                rhs_scale=x_s[a][:, m0:m1],
                start=(a == 0),
                stop=(a == r_passes - 1),
            )

        def first_scores(y):
            for m0, m1, tag, bufs in ((0, PAIR, "acc", 6), (PAIR, EARLY, "spare", 2), (EARLY, V, "spare", 2)):
                acc = psum.tile([P, m1 - m0], F32, tag=tag, bufs=bufs, name="acc")
                for m in range(m0, m1, LATE):
                    for a in range(r_passes):
                        second_pass(acc[:, m - m0 : m - m0 + LATE], 0, a, m, m + LATE)
                nc.scalar.copy(y[:, m0:m1], acc[:])

        def scores(c, y):
            acc = psum.tile([P, V], F32, tag="acc", bufs=6, name="acc")
            for a in range(r_passes):
                second_pass(acc[:], c, a, 0, V)
            nc.scalar.copy(y[:, :V], acc[:])

        def spread(c, j0, j1):
            y = y_tiles[c % Y_TILES]
            if c == 0:
                first_scores(y)
            elif j0 == 0:
                scores(c, y)
            up = ring.tile([P, j1 - j0], F32, tag="narrow", bufs=UP_BUFS, name="up")
            pick(up[:], y[:], pos3_sb, j0, j1)
            return up

        def finish(up, c, j0, j1):
            nc.vector.scalar_tensor_tensor(
                up[:], h_rows[c][:, j0:j1], vec_cols[:, PACK + c : PACK + c + 1], up[:], ALU.mult, ALU.max
            )
            nc.sync.dma_start(out[c * P : (c + 1) * P, j0:j1], up[:])

        pieces = [(c, 0, S) for c in range(tiles - 1)]
        pieces.extend((tiles - 1, j0, j1) for j0, j1 in zip(LAST_CUTS, LAST_CUTS[1:]))
        ahead = spread(*pieces[0])
        for piece, following in zip(pieces, pieces[1:] + [None]):
            up = ahead
            if following is not None:
                ahead = spread(*following)
            finish(up, *piece)
